import numpy as np
import ml_dtypes


def mxq(x, axis, fmt="e4m3"):
    dtype, down = {"e4m3": (ml_dtypes.float8_e4m3fn, 7), "e5m2": (ml_dtypes.float8_e5m2, 14)}[fmt]
    v = np.moveaxis(np.asarray(x, np.float32).astype(ml_dtypes.bfloat16).astype(np.float64), axis, -1)
    blocks = v.reshape(v.shape[:-1] + (-1, 32))
    amax = np.abs(blocks).max(-1, keepdims=True)
    byte = np.maximum(np.where(amax > 0, np.frexp(amax)[1] - 1 + 127, 0) - down, 1)
    scale = np.exp2(byte - 127.0)
    codes = (blocks / scale).astype(np.float32).astype(dtype).astype(np.float64)
    return np.moveaxis((codes * scale).reshape(v.shape), -1, axis)


WIDE = False


def mx_kscale(k):
    if not WIDE:
        return np.ones(k)
    levels = np.array([10, -10, 5, -5, 0])
    if k % 512:
        return np.exp2(np.random.permutation(np.resize(levels, k // 32))).repeat(32)
    a = np.empty((k // 512, 16))
    for p in range(k // 512):
        a[p, :8] = np.random.permutation(np.resize(levels, 8))
        for g in range(8):
            far = levels[np.abs(levels - a[p, g]) >= 10]
            a[p, g + 8] = far[np.random.randint(len(far))]
    return np.exp2(a.ravel()).repeat(32)


def f64(x):
    return np.asarray(x).astype(np.float64)


def striped(idx):
    return np.tile(idx.reshape(-1, 16).T, (8, 1)).astype(np.uint16)


def unstriped(offs):
    return offs[:16].T.reshape(-1).astype(np.int64)


def striped8(idx):
    return np.concatenate([x.reshape(-1, 16).T for x in idx]).astype(np.uint16)


def runs(offs, k):
    lists = np.stack([offs[16 * r : 16 * r + 16].T.reshape(-1) for r in range(8)]).astype(np.int64)
    return lists[np.arange(k) % 512 // 64]


def pack_weight(w):
    k, n = w.shape
    w = f64(np.asarray(w, np.float32).astype(ml_dtypes.bfloat16)).reshape(k // 32, 32, n)
    amax = np.abs(w).max(1)
    byte = np.clip(np.where(amax > 0, np.frexp(amax)[1] - 1 + 127 - 7, 1), 1, 254)
    scaled = (w * np.exp2(127.0 - byte)[:, None, :]).reshape(k, n).astype(np.float32)
    words = np.ascontiguousarray(scaled.reshape(k // 512, 128, 4, n).transpose(0, 1, 3, 2)).astype(ml_dtypes.float8_e4m3fn).view(np.uint8)
    return words, np.ascontiguousarray(byte.astype(np.uint8).reshape(k // 512, 16, n))


def unpack_weight(words, scales):
    g, p, n, _ = words.shape
    vals = np.ascontiguousarray(words).view(ml_dtypes.float8_e4m3fn).astype(np.float64) * np.repeat(np.exp2(scales.astype(np.float64) - 127.0), 8, axis=1)[..., None]
    return vals.transpose(0, 1, 3, 2).reshape(g * 512, n)


def relu(v):
    return np.maximum(v, 0.0)


K, T, S, N, H, W = 512, 2048, 512, 512, 512, 2048


def setup_inputs():
    n = np.random.standard_normal
    s = mx_kscale(K)[:, None]
    u = mx_kscale(H)
    packed_xT = pack_weight(n((K, T)) * s)
    return {
        "x_words": packed_xT[0],
        "x_scales": packed_xT[1],
        "w1": (n((K, H)) / np.sqrt(K) / s).astype(np.float32),
        "w2": (n((K, H)) / np.sqrt(K) / s).astype(np.float32),
        "gn": (np.random.uniform(0.5, 1.5, (H, 1)) * u[:, None]).astype(np.float32),
        "gm": (np.random.uniform(0.5, 1.5, (H, 1)) * u[:, None]).astype(np.float32),
        "w3": (n((H, N)) / np.sqrt(2 * H) / u[:, None]).astype(np.float32),
        "w4": (n((H, N)) / np.sqrt(2 * H) / u[:, None]).astype(np.float32),
        "offs": striped(np.random.permutation(T)[:S]),
        "hz": striped8(np.random.randint(0, T, (8, S))),
        "n1": striped(np.random.permutation(S)),
        "n2": striped(np.random.permutation(S)),
        "n3": striped(np.random.permutation(S)),
        "n4": striped(np.random.permutation(S)),
        "n5": striped(np.random.permutation(S)),
        "n6": striped(np.random.randint(0, S, W)),
    }


def reference(x_words, x_scales, w1, w2, gn, gm, w3, w4, offs, hz, n1, n2, n3, n4, n5, n6):
    xq = unpack_weight(x_words, x_scales)[:, unstriped(offs)]
    y = mxq(f64(w1), 0, "e4m3").T @ xq
    rl = relu(y)
    ds = np.zeros((H, S))
    ds[:, unstriped(n1)] = rl
    z = f64(gn) * (ds - (0.5 * y))
    x_hz = unpack_weight(x_words, x_scales)[np.arange(K)[:, None], runs(hz, K)]
    d = mxq(f64(w2), 0, "e4m3").T @ x_hz
    z2 = f64(gm) * (0.75 * (d[:, unstriped(n2)] * d[:, unstriped(n3)] - (d[:, unstriped(n4)] * d[:, unstriped(n5)])))
    h = mxq(f64(w3), 0, "e4m3").T @ mxq(z, 0, "e4m3") + mxq(f64(w4), 0, "e4m3").T @ mxq(z2, 0, "e4m3")
    mb = h[:, unstriped(n6)]
    mx = mb.reshape(N, S, 4).max(axis=2)
    mn = mb.reshape(N, S, 4).min(axis=2)
    return np.maximum(np.minimum(1.5 * h, mx), mn)

@@ -1,0 +1,273 @@
+from contextlib import ExitStack
+
+import concourse.mybir as mybir
+
+K, T, S, N, H, W = 512, 2048, 512, 512, 512, 2048
+FLOPS = 4 * 2 * 512 * 512 * 512
+
+F32 = mybir.dt.float32
+BF16 = mybir.dt.bfloat16
+I32 = mybir.dt.int32
+U32 = mybir.dt.uint32
+U16 = mybir.dt.uint16
+U8 = mybir.dt.uint8
+FP8X4 = mybir.dt.float8_e4m3fn_x4
+ALU = mybir.AluOpType
+COPY = mybir.ActivationFunctionType.Copy
+
+P = 128
+PACK = 4
+HALF = 256
+WIN = S + 32
+SHARE = 192
+
+
+def tile_picked_hjoinsenddetgclip_none_p_kernel(
+    tc, x_words, x_scales, w1, w2, gn, gm, w3, w4, offs, hz, n1, n2, n3, n4, n5, n6, out
+):
+    nc = tc.nc
+    with ExitStack() as ctx:
+        keep = ctx.enter_context(tc.tile_pool(name="keep", bufs=1))
+        ring = ctx.enter_context(tc.tile_pool(name="ring", bufs=4))
+        psum = ctx.enter_context(tc.psum_pool(name="psum", bufs=1))
+
+        def load_list(src, name):
+            tile = keep.tile(list(src.shape), U16, name=name)
+            nc.sync.dma_start(tile[:], src)
+            return tile
+
+        def sb(shape, dtype, name, tag=None):
+            return keep.tile(shape, dtype, name=name, tag=tag or name, align_bytes=64)
+
+        def load_weight(w, name):
+            raw = sb([P, PACK, H], F32, name)
+            nc.sync.dma_start(raw[:], w.rearrange("(p j) c -> p j c", j=PACK))
+            return raw
+
+        xs = sb([P, T], U8, "xs")
+        scale_rows = x_scales[0].bitcast(I32)
+        for q in range(4):
+            nc.sync.dma_start(
+                xs[32 * q : 32 * (q + 1), :].bitcast(I32),
+                scale_rows[4 * q : 4 * (q + 1), :].unsqueeze(0).to_broadcast([8, 4, T // 4]),
+            )
+        hz_t = load_list(hz, "hz_t")
+        offs_t = load_list(offs, "offs_t")
+        w1_raw = load_weight(w1, "w1_raw")
+        xw = sb([P, T], U32, "xw")
+        nc.sync.dma_start(xw[:].bitcast(I32), x_words[0].rearrange("p n t -> p (n t)").bitcast(I32))
+        gn_t = sb([P, PACK], F32, "gn_t")
+        nc.sync.dma_start(gn_t[:], gn.rearrange("(p t) o -> p (t o)", t=PACK))
+        n1_t = load_list(n1, "n1_t")
+        w2_raw = load_weight(w2, "w2_raw")
+        gm_t = sb([P, PACK], F32, "gm_t")
+        nc.sync.dma_start(gm_t[:], gm.rearrange("(p t) o -> p (t o)", t=PACK))
+        n2_t = load_list(n2, "n2_t")
+        n3_t = load_list(n3, "n3_t")
+        n4_t = load_list(n4, "n4_t")
+
+        d_win = [sb([P, WIN], F32, "d_win%d" % t) for t in range(PACK)]
+        dg_win = [sb([P, WIN], F32, "dg_win%d" % t) for t in range(PACK)]
+        h_win = [sb([P, WIN], F32, "h_win%d" % t) for t in range(PACK)]
+        for win in d_win + dg_win + h_win:
+            nc.gpsimd.memset(win[:, S:WIN], 0.0)
+
+        gn_half = sb([P, PACK], F32, "gn_half")
+        gm75 = sb([P, PACK], F32, "gm75")
+        nc.gpsimd.tensor_scalar(gn_half[:], gn_t[:], -0.5, 0.0, ALU.mult, ALU.add)
+        nc.gpsimd.tensor_scalar(gm75[:], gm_t[:], 0.75, 0.0, ALU.mult, ALU.add)
+
+        hz_bytes = sb([P, S], U8, "hz_bytes")
+        nc.vector.tensor_copy(hz_bytes[:], xs[:].indirect(hz_t[:]))
+        xh_scale = sb([P, S], U8, "xh_scale")
+        nc.vector.tensor_copy(xh_scale[:].bitcast(I32), hz_bytes[:].bitcast(I32))
+        xq_scale = sb([P, S], U8, "xq_scale")
+        nc.vector.tensor_copy(xq_scale[:], xs[:].indirect(offs_t[:]))
+        for r in range(2):
+            nc.sync.dma_start(xh_scale[2 + r : P : 32, :].bitcast(I32), hz_bytes[18 + r : P : 32, :].bitcast(I32))
+        w4_raw = load_weight(w4, "w4_raw")
+        n5_t = load_list(n5, "n5_t")
+        w3_raw = load_weight(w3, "w3_raw")
+        n6_t = load_list(n6, "n6_t")
+        xq_code = sb([P, S], U32, "xq_code")
+        nc.vector.tensor_copy(xq_code[:], xw[:].indirect(offs_t[:]))
+        xh_code = sb([P, S], U32, "xh_code")
+        nc.vector.tensor_copy(xh_code[:], xw[:].indirect(hz_t[:]))
+
+        def quantize(src, name):
+            code = sb([P, src.shape[1] // PACK], U32, name + "_code")
+            scale = sb([P, src.shape[1] // PACK], U8, name + "_scale")
+            nc.vector.quantize_mx(out=code[:].bitcast(FP8X4), scales=scale[:], in_=src)
+            return code, scale
+
+        def mm(acc, lhs, cols, rhs, start, stop):
+            nc.tensor.matmul_mx(
+                out=acc,
+                lhsT=lhs[0][:, cols].bitcast(FP8X4),
+                lhsT_scale=lhs[1][:, cols],
+                rhs=rhs[0][:].bitcast(FP8X4),
+                rhs_scale=rhs[1][:],
+                start=start,
+                stop=stop,
+            )
+
+        w1_bf = sb([P, H * PACK], BF16, "w1_bf")
+        w1_view = w1_bf[:].rearrange("p (t m j) -> p m j t", t=PACK, j=PACK)
+        w1_src = w1_raw[:].rearrange("p j (m t) -> p m j t", t=PACK)
+        nc.scalar.copy(w1_view[:, 0:64], w1_src[:, 0:64])
+        nc.vector.tensor_copy(w1_view[:, 64:128], w1_src[:, 64:128])
+        y_acc = []
+        rl = sb([P, PACK, S], F32, "rl")
+        w1_q = [quantize(w1_bf[:, u * 1024 : (u + 1) * 1024], "w1_%d" % u) for u in range(2)]
+        for t in range(PACK):
+            acc = psum.tile([P, S], F32, name="y%d" % t, tag="bankA%d" % t)
+            mm(acc[:], w1_q[t // 2], slice((t % 2) * P, (t % 2 + 1) * P), (xq_code, xq_scale), True, True)
+            nc.vector.tensor_scalar(rl[:, t, :], acc[:], 0.0, gn_t[:, t : t + 1], ALU.max, ALU.mult)
+            y_acc.append(acc)
+
+        w2_bf = sb([P, H * PACK], BF16, "w2_bf")
+        nc.scalar.copy(
+            w2_bf[:].rearrange("p (t m j) -> p m j t", t=PACK, j=PACK),
+            w2_raw[:].rearrange("p j (m t) -> p m j t", t=PACK),
+        )
+        w2_q = quantize(w2_bf[:], "w2")
+
+        def scatter(ds, t, start, count, on_vector):
+            lists = n1_t[:, start // 16 : (start + count) // 16]
+            src = rl[:, t, start : start + count]
+            if on_vector:
+                nc.vector.tensor_copy(ds[:].indirect(lists), src)
+            else:
+                nc.scalar.activation(ds[:].indirect(lists), src, COPY)
+
+        ds0 = sb([P, S], F32, "ds0", tag="w2_raw")
+        scatter(ds0, 0, 0, HALF, False)
+        scatter(ds0, 0, HALF, HALF, False)
+
+        for t in range(PACK):
+            acc = psum.tile([P, S], F32, name="d%d" % t, tag="bankB%d" % t)
+            mm(acc[:], w2_q, slice(t * P, (t + 1) * P), (xh_code, xh_scale), True, True)
+            if t < 2:
+                nc.vector.tensor_copy(d_win[t][:, 0:S], acc[:])
+            else:
+                nc.scalar.copy(d_win[t][:, 0:S], acc[:])
+        for t in range(PACK):
+            nc.vector.tensor_scalar(dg_win[t][:, 0:S], d_win[t][:, 0:S], gm75[:, t : t + 1], None, ALU.mult)
+
+        def cast_plain(raw, name):
+            bf = sb([P, H * PACK], BF16, name)
+            nc.vector.tensor_copy(
+                bf[:].rearrange("p (c i j) -> p c j i", i=4, j=PACK),
+                raw[:].rearrange("p j (c i) -> p c j i", i=4),
+            )
+            return bf
+
+        w4_bf = cast_plain(w4_raw, "w4_bf")
+        w3_bf = cast_plain(w3_raw, "w3_bf")
+        w4_q = quantize(w4_bf[:], "w4")
+        w3_q = quantize(w3_bf[:], "w3")
+
+        ab = sb([P, PACK, S], F32, "ab")
+        ce = sb([P, PACK, S], F32, "ce")
+        for t in range(PACK):
+            for first, second, prod in ((n2_t, n3_t, ab), (n4_t, n5_t, ce)):
+                left = ring.tile([P, S], F32, name="left", bufs=8)
+                nc.scalar.activation(left[:], dg_win[t][:].indirect(first[:]), COPY)
+                nc.vector.tensor_tensor(prod[:, t, :], d_win[t][:].indirect(second[:]), left[:], ALU.mult)
+
+        halves = [slice(u * HALF, (u + 1) * HALF) for u in range(2)]
+        z2_bf = sb([P, S * PACK], BF16, "z2_bf")
+        for u in range(2):
+            nc.vector.tensor_tensor(
+                z2_bf[:, u * 1024 : (u + 1) * 1024].rearrange("p (c i t) -> p c t i", i=4, t=PACK),
+                ab[:, :, halves[u]].rearrange("p t (c i) -> p c t i", i=4),
+                ce[:, :, halves[u]].rearrange("p t (c i) -> p c t i", i=4),
+                ALU.subtract,
+            )
+        z2_q = [quantize(z2_bf[:, u * 1024 : (u + 1) * 1024], "z2_%d" % u) for u in range(2)]
+
+        zp = sb([P, PACK, S], BF16, "zp", tag="z2_bf")
+
+        def z_plane(ds, t, cols):
+            nc.vector.scalar_tensor_tensor(
+                zp[:, t, cols], y_acc[t][:, cols], gn_half[:, t : t + 1], ds[:, cols], ALU.mult, ALU.add
+            )
+
+        ds1 = sb([P, S], F32, "ds1", tag="dg_win1")
+        ds2 = sb([P, S], F32, "ds2", tag="dg_win2")
+        ds3 = sb([P, S], F32, "ds3", tag="dg_win3")
+        scatter(ds3, 3, 0, SHARE, True)
+        scatter(ds1, 1, 0, HALF, False)
+        scatter(ds1, 1, HALF, HALF, False)
+        scatter(ds2, 2, 0, HALF, False)
+        scatter(ds2, 2, HALF, HALF, False)
+        scatter(ds3, 3, SHARE, S - SHARE, False)
+        for t, ds in enumerate((ds0, ds1, ds2)):
+            z_plane(ds, t, slice(0, S))
+        for cols in halves:
+            z_plane(ds3, 3, cols)
+        z_bf = [sb([P, HALF * PACK], BF16, "z_bf%d" % u) for u in range(2)]
+        for u in range(2):
+            nc.vector.tensor_copy(
+                z_bf[u][:].rearrange("p (c i t) -> p c t i", i=4, t=PACK),
+                zp[:, :, halves[u]].rearrange("p t (c i) -> p c t i", i=4),
+            )
+        z_q = [quantize(z_bf[u][:], "z_%d" % u) for u in range(2)]
+
+        accs = {}
+        for m in range(PACK):
+            for u in range(2):
+                acc = psum.tile([P, HALF], F32, name="h%d_%d" % (m, u), tag="bank%s%d" % ("BA"[u], m))
+                cols = slice(m * P, (m + 1) * P)
+                mm(acc[:], w4_q, cols, z2_q[u], True, False)
+                mm(acc[:], w3_q, cols, z_q[u], False, True)
+                accs[m, u] = acc
+
+        def leave(m, u, on_vector):
+            if on_vector:
+                nc.vector.tensor_copy(h_win[m][:, halves[u]], accs[m, u][:])
+            else:
+                nc.scalar.copy(h_win[m][:, halves[u]], accs[m, u][:])
+
+        def fetch(m, start, count, on_vector):
+            dst = members[m][:, start : start + count, :].rearrange("p j e -> p (j e)")
+            lists = n6_t[:, start // 4 : (start + count) // 4]
+            if on_vector:
+                nc.vector.tensor_copy(dst, h_win[m][:].indirect(lists))
+            else:
+                nc.scalar.activation(dst, h_win[m][:].indirect(lists), COPY)
+
+        def clip(m, start, count):
+            cols = slice(start, start + count)
+            mb = members[m][:, cols, :]
+            hi2 = ring.tile([P, count, 2], F32, name="hi2", bufs=2)
+            lo2 = ring.tile([P, count, 2], F32, name="lo2", bufs=2)
+            mx = ring.tile([P, count], F32, name="mx", bufs=2)
+            mn = ring.tile([P, count], F32, name="mn", bufs=2)
+            cap = ring.tile([P, count], F32, name="cap", bufs=2)
+            res = ring.tile([P, count], F32, name="res", bufs=3)
+            nc.vector.tensor_tensor(hi2[:], mb[:, :, 0:2], mb[:, :, 2:4], ALU.max)
+            nc.vector.tensor_tensor(lo2[:], mb[:, :, 0:2], mb[:, :, 2:4], ALU.min)
+            nc.vector.tensor_tensor(mx[:], hi2[:, :, 0], hi2[:, :, 1], ALU.max)
+            nc.vector.tensor_tensor(mn[:], lo2[:, :, 0], lo2[:, :, 1], ALU.min)
+            nc.vector.scalar_tensor_tensor(cap[:], h_win[m][:, cols], 1.5, mx[:], ALU.mult, ALU.min)
+            nc.vector.tensor_tensor(res[:], cap[:], mn[:], ALU.max)
+            nc.sync.dma_start(out[m * P : (m + 1) * P, cols], res[:])
+
+        members = [ring.tile([P, S, 4], F32, name="members%d" % m, tag="members", bufs=3) for m in range(PACK)]
+        batches = [(P, P, HALF), (HALF, HALF), (HALF, HALF), (HALF, P, P)]
+        leave(0, 0, False)
+        leave(0, 1, True)
+        for m in (1, 2):
+            leave(m, 0, True)
+            leave(m, 1, True)
+        for m in range(PACK):
+            start = 0
+            for count in batches[m]:
+                for piece in range(start, start + count, P):
+                    fetch(m, piece, P, False)
+                if start == 0 and m == 2:
+                    leave(m + 1, 0, False)
+                    leave(m + 1, 1, False)
+                clip(m, start, count)
+                start += count

@@ -19,7 +19,8 @@ P = 128
 PACK = 4
 HALF = 256
 WIN = S + 32
-SHARE = 192
+SHARE = 224
+EARLY = 256
 
 
 def tile_picked_hjoinsenddetgclip_none_p_kernel(
@@ -39,8 +40,8 @@ def tile_picked_hjoinsenddetgclip_none_p_kernel(
         def sb(shape, dtype, name, tag=None):
             return keep.tile(shape, dtype, name=name, tag=tag or name, align_bytes=64)
 
-        def load_weight(w, name):
-            raw = sb([P, PACK, H], F32, name)
+        def load_weight(w, name, tag=None):
+            raw = sb([P, PACK, H], F32, name, tag=tag)
             nc.sync.dma_start(raw[:], w.rearrange("(p j) c -> p j c", j=PACK))
             return raw
 
@@ -53,16 +54,16 @@ def tile_picked_hjoinsenddetgclip_none_p_kernel(
             )
         hz_t = load_list(hz, "hz_t")
         offs_t = load_list(offs, "offs_t")
-        w1_raw = load_weight(w1, "w1_raw")
-        xw = sb([P, T], U32, "xw")
-        nc.sync.dma_start(xw[:].bitcast(I32), x_words[0].rearrange("p n t -> p (n t)").bitcast(I32))
         gn_t = sb([P, PACK], F32, "gn_t")
         nc.sync.dma_start(gn_t[:], gn.rearrange("(p t) o -> p (t o)", t=PACK))
+        xw = sb([P, T], U32, "xw")
+        nc.sync.dma_start(xw[:].bitcast(I32), x_words[0].rearrange("p n t -> p (n t)").bitcast(I32))
+        w1_raw = load_weight(w1, "w1_raw")
         n1_t = load_list(n1, "n1_t")
-        w2_raw = load_weight(w2, "w2_raw")
         gm_t = sb([P, PACK], F32, "gm_t")
         nc.sync.dma_start(gm_t[:], gm.rearrange("(p t) o -> p (t o)", t=PACK))
         n2_t = load_list(n2, "n2_t")
+        w2_raw = load_weight(w2, "w2_raw")
         n3_t = load_list(n3, "n3_t")
         n4_t = load_list(n4, "n4_t")
 
@@ -74,8 +75,8 @@ def tile_picked_hjoinsenddetgclip_none_p_kernel(
 
         gn_half = sb([P, PACK], F32, "gn_half")
         gm75 = sb([P, PACK], F32, "gm75")
-        nc.gpsimd.tensor_scalar(gn_half[:], gn_t[:], -0.5, 0.0, ALU.mult, ALU.add)
-        nc.gpsimd.tensor_scalar(gm75[:], gm_t[:], 0.75, 0.0, ALU.mult, ALU.add)
+        nc.scalar.activation(gn_half[:], gn_t[:], COPY, scale=-0.5)
+        nc.scalar.activation(gm75[:], gm_t[:], COPY, scale=0.75)
 
         hz_bytes = sb([P, S], U8, "hz_bytes")
         nc.vector.tensor_copy(hz_bytes[:], xs[:].indirect(hz_t[:]))
@@ -85,17 +86,16 @@ def tile_picked_hjoinsenddetgclip_none_p_kernel(
         nc.vector.tensor_copy(xq_scale[:], xs[:].indirect(offs_t[:]))
         for r in range(2):
             nc.sync.dma_start(xh_scale[2 + r : P : 32, :].bitcast(I32), hz_bytes[18 + r : P : 32, :].bitcast(I32))
-        w4_raw = load_weight(w4, "w4_raw")
         n5_t = load_list(n5, "n5_t")
-        w3_raw = load_weight(w3, "w3_raw")
         n6_t = load_list(n6, "n6_t")
+
         xq_code = sb([P, S], U32, "xq_code")
         nc.vector.tensor_copy(xq_code[:], xw[:].indirect(offs_t[:]))
         xh_code = sb([P, S], U32, "xh_code")
         nc.vector.tensor_copy(xh_code[:], xw[:].indirect(hz_t[:]))
 
-        def quantize(src, name):
-            code = sb([P, src.shape[1] // PACK], U32, name + "_code")
+        def quantize(src, name, tag=None):
+            code = sb([P, src.shape[1] // PACK], U32, name + "_code", tag=tag)
             scale = sb([P, src.shape[1] // PACK], U8, name + "_scale")
             nc.vector.quantize_mx(out=code[:].bitcast(FP8X4), scales=scale[:], in_=src)
             return code, scale
@@ -111,30 +111,41 @@ def tile_picked_hjoinsenddetgclip_none_p_kernel(
                 stop=stop,
             )
 
-        w1_bf = sb([P, H * PACK], BF16, "w1_bf")
-        w1_view = w1_bf[:].rearrange("p (t m j) -> p m j t", t=PACK, j=PACK)
-        w1_src = w1_raw[:].rearrange("p j (m t) -> p m j t", t=PACK)
-        nc.scalar.copy(w1_view[:, 0:64], w1_src[:, 0:64])
-        nc.vector.tensor_copy(w1_view[:, 64:128], w1_src[:, 64:128])
+        def cast_dealt(raw, name, copies):
+            src = raw[:].rearrange("p j (m t) -> p m j t", t=PACK)
+            parts = [sb([P, 2 * P * PACK], BF16, "%s%d" % (name, u)) for u in range(2)]
+            for u, copy in enumerate(copies):
+                copy(parts[u][:].rearrange("p (t m j) -> p m j t", t=2, j=PACK), src[:, :, :, 2 * u : 2 * u + 2])
+            return parts
+
+        w1_bf = cast_dealt(w1_raw, "w1_bf", (nc.scalar.copy, nc.vector.tensor_copy))
+        w1_q = [quantize(w1_bf[0][:], "w1_0"), quantize(w1_bf[1][:], "w1_1", tag="w1_bf0")]
+        w4_raw = load_weight(w4, "w4_raw", tag="w1_raw")
+        w3_raw = load_weight(w3, "w3_raw", tag="w1_bf1")
         y_acc = []
-        rl = sb([P, PACK, S], F32, "rl")
-        w1_q = [quantize(w1_bf[:, u * 1024 : (u + 1) * 1024], "w1_%d" % u) for u in range(2)]
         for t in range(PACK):
             acc = psum.tile([P, S], F32, name="y%d" % t, tag="bankA%d" % t)
             mm(acc[:], w1_q[t // 2], slice((t % 2) * P, (t % 2 + 1) * P), (xq_code, xq_scale), True, True)
-            nc.vector.tensor_scalar(rl[:, t, :], acc[:], 0.0, gn_t[:, t : t + 1], ALU.max, ALU.mult)
             y_acc.append(acc)
+        rl = {}
 
-        w2_bf = sb([P, H * PACK], BF16, "w2_bf")
-        nc.scalar.copy(
-            w2_bf[:].rearrange("p (t m j) -> p m j t", t=PACK, j=PACK),
-            w2_raw[:].rearrange("p j (m t) -> p m j t", t=PACK),
-        )
-        w2_q = quantize(w2_bf[:], "w2")
+        def gained_relu(t, dst):
+            rl[t] = dst
+            nc.vector.tensor_scalar(dst, y_acc[t][:], 0.0, gn_t[:, t : t + 1], ALU.max, ALU.mult)
+
+        rl0 = sb([P, S], F32, "rl0")
+        gained_relu(0, rl0[:])
+        w2_bf = cast_dealt(w2_raw, "w2_bf", (nc.vector.tensor_copy, nc.scalar.copy))
+        w2_q = [quantize(w2_bf[u][:], "w2_%d" % u) for u in range(2)]
+        rl1 = sb([P, S], F32, "rl1", tag="w2_bf0")
+        rl23 = sb([P, 2, S], F32, "rl23", tag="w2_bf1")
+        gained_relu(1, rl1[:])
+        gained_relu(2, rl23[:, 0, :])
+        gained_relu(3, rl23[:, 1, :])
 
         def scatter(ds, t, start, count, on_vector):
             lists = n1_t[:, start // 16 : (start + count) // 16]
-            src = rl[:, t, start : start + count]
+            src = rl[t][:, start : start + count]
             if on_vector:
                 nc.vector.tensor_copy(ds[:].indirect(lists), src)
             else:
@@ -146,35 +157,39 @@ def tile_picked_hjoinsenddetgclip_none_p_kernel(
 
         for t in range(PACK):
             acc = psum.tile([P, S], F32, name="d%d" % t, tag="bankB%d" % t)
-            mm(acc[:], w2_q, slice(t * P, (t + 1) * P), (xh_code, xh_scale), True, True)
+            mm(acc[:], w2_q[t // 2], slice((t % 2) * P, (t % 2 + 1) * P), (xh_code, xh_scale), True, True)
             if t < 2:
                 nc.vector.tensor_copy(d_win[t][:, 0:S], acc[:])
             else:
                 nc.scalar.copy(d_win[t][:, 0:S], acc[:])
-        for t in range(PACK):
+
+        def cast_plain(copy, bf, raw):
+            copy(bf.rearrange("p (c i j) -> p c j i", i=4, j=PACK), raw.rearrange("p j (c i) -> p c j i", i=4))
+
+        def gained_d(t):
             nc.vector.tensor_scalar(dg_win[t][:, 0:S], d_win[t][:, 0:S], gm75[:, t : t + 1], None, ALU.mult)
 
-        def cast_plain(raw, name):
-            bf = sb([P, H * PACK], BF16, name)
-            nc.vector.tensor_copy(
-                bf[:].rearrange("p (c i j) -> p c j i", i=4, j=PACK),
-                raw[:].rearrange("p j (c i) -> p c j i", i=4),
-            )
-            return bf
-
-        w4_bf = cast_plain(w4_raw, "w4_bf")
-        w3_bf = cast_plain(w3_raw, "w3_bf")
-        w4_q = quantize(w4_bf[:], "w4")
-        w3_q = quantize(w3_bf[:], "w3")
+        for t in range(2):
+            gained_d(t)
+        w4_early_bf = sb([P, EARLY * PACK], BF16, "w4_early_bf")
+        cast_plain(nc.vector.tensor_copy, w4_early_bf[:], w4_raw[:, :, 0:EARLY])
+        for t in range(2, PACK):
+            gained_d(t)
+        w4_early_q = quantize(w4_early_bf[:], "w4_early")
 
         ab = sb([P, PACK, S], F32, "ab")
         ce = sb([P, PACK, S], F32, "ce")
         for t in range(PACK):
             for first, second, prod in ((n2_t, n3_t, ab), (n4_t, n5_t, ce)):
-                left = ring.tile([P, S], F32, name="left", bufs=8)
+                left = ring.tile([P, S], F32, name="left", bufs=8, align_bytes=64)
                 nc.scalar.activation(left[:], dg_win[t][:].indirect(first[:]), COPY)
                 nc.vector.tensor_tensor(prod[:, t, :], d_win[t][:].indirect(second[:]), left[:], ALU.mult)
 
+        w3_early_bf = ring.tile([P, EARLY * PACK], BF16, name="w3_early_bf", tag="left", bufs=8, align_bytes=64)
+        cast_plain(nc.vector.tensor_copy, w3_early_bf[:], w3_raw[:, :, 0:EARLY])
+        ds3 = sb([P, S], F32, "ds3", tag="dg_win3")
+        scatter(ds3, 3, 0, SHARE, True)
+        w3_early_q = quantize(w3_early_bf[:], "w3_early")
         halves = [slice(u * HALF, (u + 1) * HALF) for u in range(2)]
         z2_bf = sb([P, S * PACK], BF16, "z2_bf")
         for u in range(2):
@@ -195,13 +210,14 @@ def tile_picked_hjoinsenddetgclip_none_p_kernel(
 
         ds1 = sb([P, S], F32, "ds1", tag="dg_win1")
         ds2 = sb([P, S], F32, "ds2", tag="dg_win2")
-        ds3 = sb([P, S], F32, "ds3", tag="dg_win3")
-        scatter(ds3, 3, 0, SHARE, True)
         scatter(ds1, 1, 0, HALF, False)
         scatter(ds1, 1, HALF, HALF, False)
         scatter(ds2, 2, 0, HALF, False)
         scatter(ds2, 2, HALF, HALF, False)
         scatter(ds3, 3, SHARE, S - SHARE, False)
+        late_bf = sb([P, 2, (N - EARLY) * PACK], BF16, "late_bf", tag="w2_bf1")
+        cast_plain(nc.scalar.copy, late_bf[:, 0, :], w4_raw[:, :, EARLY:N])
+        cast_plain(nc.scalar.copy, late_bf[:, 1, :], w3_raw[:, :, EARLY:N])
         for t, ds in enumerate((ds0, ds1, ds2)):
             z_plane(ds, t, slice(0, S))
         for cols in halves:
@@ -213,14 +229,19 @@ def tile_picked_hjoinsenddetgclip_none_p_kernel(
                 zp[:, :, halves[u]].rearrange("p t (c i) -> p c t i", i=4),
             )
         z_q = [quantize(z_bf[u][:], "z_%d" % u) for u in range(2)]
+        late_q = quantize(late_bf[:].rearrange("p w c -> p (w c)"), "late", tag="z_bf1")
 
         accs = {}
         for m in range(PACK):
             for u in range(2):
                 acc = psum.tile([P, HALF], F32, name="h%d_%d" % (m, u), tag="bank%s%d" % ("BA"[u], m))
-                cols = slice(m * P, (m + 1) * P)
-                mm(acc[:], w4_q, cols, z2_q[u], True, False)
-                mm(acc[:], w3_q, cols, z_q[u], False, True)
+                first = (m % 2) * P
+                if m < 2:
+                    mm(acc[:], w4_early_q, slice(first, first + P), z2_q[u], True, False)
+                    mm(acc[:], w3_early_q, slice(first, first + P), z_q[u], False, True)
+                else:
+                    mm(acc[:], late_q, slice(first, first + P), z2_q[u], True, False)
+                    mm(acc[:], late_q, slice(HALF + first, HALF + first + P), z_q[u], False, True)
                 accs[m, u] = acc
 
         def leave(m, u, on_vector):
@@ -255,18 +276,18 @@ def tile_picked_hjoinsenddetgclip_none_p_kernel(
             nc.sync.dma_start(out[m * P : (m + 1) * P, cols], res[:])
 
         members = [ring.tile([P, S, 4], F32, name="members%d" % m, tag="members", bufs=3) for m in range(PACK)]
-        batches = [(P, P, HALF), (HALF, HALF), (HALF, HALF), (HALF, P, P)]
+        batches = [(HALF, HALF), (HALF, HALF), (HALF, HALF), (HALF, HALF)]
         leave(0, 0, False)
         leave(0, 1, True)
-        for m in (1, 2):
-            leave(m, 0, True)
-            leave(m, 1, True)
+        leave(1, 0, False)
         for m in range(PACK):
             start = 0
             for count in batches[m]:
                 for piece in range(start, start + count, P):
-                    fetch(m, piece, P, False)
-                if start == 0 and m == 2:
+                    fetch(m, piece, P, m == 0 and piece == P)
+                if start == 0 and m == 0:
+                    leave(1, 1, False)
+                if start == 0 and m in (1, 2):
                     leave(m + 1, 0, False)
                     leave(m + 1, 1, False)
                 clip(m, start, count)

@@ -164,7 +164,7 @@ def tile_picked_hjoinsenddetgclip_none_p_kernel(
                 nc.scalar.copy(d_win[t][:, 0:S], acc[:])
 
         def cast_plain(copy, bf, raw):
-            copy(bf.rearrange("p (c i j) -> p c j i", i=4, j=PACK), raw.rearrange("p j (c i) -> p c j i", i=4))
+            copy(bf.rearrange("p (c i j) -> p c j i", i=2, j=PACK), raw.rearrange("p j (c i) -> p c j i", i=2))
 
         def gained_d(t):
             nc.vector.tensor_scalar(dg_win[t][:, 0:S], d_win[t][:, 0:S], gm75[:, t : t + 1], None, ALU.mult)
@@ -189,17 +189,17 @@ def tile_picked_hjoinsenddetgclip_none_p_kernel(
         cast_plain(nc.vector.tensor_copy, w3_early_bf[:], w3_raw[:, :, 0:EARLY])
         ds3 = sb([P, S], F32, "ds3", tag="dg_win3")
         scatter(ds3, 3, 0, SHARE, True)
-        w3_early_q = quantize(w3_early_bf[:], "w3_early")
         halves = [slice(u * HALF, (u + 1) * HALF) for u in range(2)]
         z2_bf = sb([P, S * PACK], BF16, "z2_bf")
-        for u in range(2):
-            nc.vector.tensor_tensor(
-                z2_bf[:, u * 1024 : (u + 1) * 1024].rearrange("p (c i t) -> p c t i", i=4, t=PACK),
-                ab[:, :, halves[u]].rearrange("p t (c i) -> p c t i", i=4),
-                ce[:, :, halves[u]].rearrange("p t (c i) -> p c t i", i=4),
-                ALU.subtract,
-            )
-        z2_q = [quantize(z2_bf[:, u * 1024 : (u + 1) * 1024], "z2_%d" % u) for u in range(2)]
+        nc.vector.tensor_tensor(
+            z2_bf[:].rearrange("p (c i t) -> p c t i", i=2, t=PACK),
+            ab[:].rearrange("p t (c i) -> p c t i", i=2),
+            ce[:].rearrange("p t (c i) -> p c t i", i=2),
+            ALU.subtract,
+        )
+        w3_early_q = quantize(w3_early_bf[:], "w3_early")
+        z2_code, z2_scale = quantize(z2_bf[:], "z2")
+        z2_q = [(z2_code[:, cols], z2_scale[:, cols]) for cols in halves]
 
         zp = sb([P, PACK, S], BF16, "zp", tag="z2_bf")
 

@@ -19,7 +19,8 @@ P = 128
 PACK = 4
 HALF = 256
 WIN = S + 32
-SHARE = 224
+H_WIN = 2 * S + 32
+SHARE = 256
 EARLY = 256
 
 
@@ -69,9 +70,9 @@ def tile_picked_hjoinsenddetgclip_none_p_kernel(
 
         d_win = [sb([P, WIN], F32, "d_win%d" % t) for t in range(PACK)]
         dg_win = [sb([P, WIN], F32, "dg_win%d" % t) for t in range(PACK)]
-        h_win = [sb([P, WIN], F32, "h_win%d" % t) for t in range(PACK)]
+        h_win = [sb([P, H_WIN], F32, "h_win%d" % t) for t in range(PACK)]
         for win in d_win + dg_win + h_win:
-            nc.gpsimd.memset(win[:, S:WIN], 0.0)
+            nc.gpsimd.memset(win[:, S : win.shape[1]], 0.0)
 
         gn_half = sb([P, PACK], F32, "gn_half")
         gm75 = sb([P, PACK], F32, "gm75")
@@ -276,19 +277,18 @@ def tile_picked_hjoinsenddetgclip_none_p_kernel(
             nc.sync.dma_start(out[m * P : (m + 1) * P, cols], res[:])
 
         members = [ring.tile([P, S, 4], F32, name="members%d" % m, tag="members", bufs=3) for m in range(PACK)]
-        batches = [(HALF, HALF), (HALF, HALF), (HALF, HALF), (HALF, HALF)]
         leave(0, 0, False)
         leave(0, 1, True)
         leave(1, 0, False)
         for m in range(PACK):
-            start = 0
-            for count in batches[m]:
-                for piece in range(start, start + count, P):
-                    fetch(m, piece, P, m == 0 and piece == P)
-                if start == 0 and m == 0:
+            for u in range(2):
+                if m == 0 and u == 0:
+                    fetch(m, 0, P, False)
+                    fetch(m, P, P, True)
                     leave(1, 1, False)
-                if start == 0 and m in (1, 2):
+                else:
+                    fetch(m, u * HALF, HALF, False)
+                if u == 0 and m in (1, 2):
                     leave(m + 1, 0, False)
-                    leave(m + 1, 1, False)
-                clip(m, start, count)
-                start += count
+                    leave(m + 1, 1, True)
+                clip(m, u * HALF, HALF)

from contextlib import ExitStack

import concourse.mybir as mybir

K, T, S, N, H, W = 512, 2048, 512, 512, 512, 2048
FLOPS = 4 * 2 * 512 * 512 * 512

F32 = mybir.dt.float32
BF16 = mybir.dt.bfloat16
I32 = mybir.dt.int32
U32 = mybir.dt.uint32
U16 = mybir.dt.uint16
U8 = mybir.dt.uint8
FP8X4 = mybir.dt.float8_e4m3fn_x4
ALU = mybir.AluOpType
COPY = mybir.ActivationFunctionType.Copy

P = 128
PACK = 4
HALF = 256
WIN = S + 32
H_WIN = 2 * S + 32
SHARE = 256
EARLY = 256


def tile_picked_hjoinsenddetgclip_none_p_kernel(
    tc, x_words, x_scales, w1, w2, gn, gm, w3, w4, offs, hz, n1, n2, n3, n4, n5, n6, out
):
    nc = tc.nc
    with ExitStack() as ctx:
        keep = ctx.enter_context(tc.tile_pool(name="keep", bufs=1))
        ring = ctx.enter_context(tc.tile_pool(name="ring", bufs=4))
        psum = ctx.enter_context(tc.psum_pool(name="psum", bufs=1))

        def load_list(src, name):
            tile = keep.tile(list(src.shape), U16, name=name)
            nc.sync.dma_start(tile[:], src)
            return tile

        def sb(shape, dtype, name, tag=None):
            return keep.tile(shape, dtype, name=name, tag=tag or name, align_bytes=64)

        def load_weight(w, name, tag=None):
            raw = sb([P, PACK, H], F32, name, tag=tag)
            nc.sync.dma_start(raw[:], w.rearrange("(p j) c -> p j c", j=PACK))
            return raw

        xs = sb([P, T], U8, "xs")
        scale_rows = x_scales[0].bitcast(I32)
        for q in range(4):
            nc.sync.dma_start(
                xs[32 * q : 32 * (q + 1), :].bitcast(I32),
                scale_rows[4 * q : 4 * (q + 1), :].unsqueeze(0).to_broadcast([8, 4, T // 4]),
            )
        hz_t = load_list(hz, "hz_t")
        offs_t = load_list(offs, "offs_t")
        gn_t = sb([P, PACK], F32, "gn_t")
        nc.sync.dma_start(gn_t[:], gn.rearrange("(p t) o -> p (t o)", t=PACK))
        xw = sb([P, T], U32, "xw")
        nc.sync.dma_start(xw[:].bitcast(I32), x_words[0].rearrange("p n t -> p (n t)").bitcast(I32))
        w1_raw = load_weight(w1, "w1_raw")
        n1_t = load_list(n1, "n1_t")
        gm_t = sb([P, PACK], F32, "gm_t")
        nc.sync.dma_start(gm_t[:], gm.rearrange("(p t) o -> p (t o)", t=PACK))
        n2_t = load_list(n2, "n2_t")
        w2_raw = load_weight(w2, "w2_raw")
        n3_t = load_list(n3, "n3_t")
        n4_t = load_list(n4, "n4_t")

        d_win = [sb([P, WIN], F32, "d_win%d" % t) for t in range(PACK)]
        dg_win = [sb([P, WIN], F32, "dg_win%d" % t) for t in range(PACK)]
        h_win = [sb([P, H_WIN], F32, "h_win%d" % t) for t in range(PACK)]
        for win in d_win + dg_win + h_win:
            nc.gpsimd.memset(win[:, S : win.shape[1]], 0.0)

        gn_half = sb([P, PACK], F32, "gn_half")
        gm75 = sb([P, PACK], F32, "gm75")
        nc.scalar.activation(gn_half[:], gn_t[:], COPY, scale=-0.5)
        nc.scalar.activation(gm75[:], gm_t[:], COPY, scale=0.75)

        hz_bytes = sb([P, S], U8, "hz_bytes")
        nc.vector.tensor_copy(hz_bytes[:], xs[:].indirect(hz_t[:]))
        xh_scale = sb([P, S], U8, "xh_scale")
        nc.vector.tensor_copy(xh_scale[:].bitcast(I32), hz_bytes[:].bitcast(I32))
        xq_scale = sb([P, S], U8, "xq_scale")
        nc.vector.tensor_copy(xq_scale[:], xs[:].indirect(offs_t[:]))
        for r in range(2):
            nc.sync.dma_start(xh_scale[2 + r : P : 32, :].bitcast(I32), hz_bytes[18 + r : P : 32, :].bitcast(I32))
        n5_t = load_list(n5, "n5_t")
        n6_t = load_list(n6, "n6_t")

        xq_code = sb([P, S], U32, "xq_code")
        nc.vector.tensor_copy(xq_code[:], xw[:].indirect(offs_t[:]))
        xh_code = sb([P, S], U32, "xh_code")
        nc.vector.tensor_copy(xh_code[:], xw[:].indirect(hz_t[:]))

        def quantize(src, name, tag=None):
            code = sb([P, src.shape[1] // PACK], U32, name + "_code", tag=tag)
            scale = sb([P, src.shape[1] // PACK], U8, name + "_scale")
            nc.vector.quantize_mx(out=code[:].bitcast(FP8X4), scales=scale[:], in_=src)
            return code, scale

        def mm(acc, lhs, cols, rhs, start, stop):
            nc.tensor.matmul_mx(
                out=acc,
                lhsT=lhs[0][:, cols].bitcast(FP8X4),
                lhsT_scale=lhs[1][:, cols],
                rhs=rhs[0][:].bitcast(FP8X4),
                rhs_scale=rhs[1][:],
                start=start,
                stop=stop,
            )

        def cast_dealt(raw, name, copies):
            src = raw[:].rearrange("p j (m t) -> p m j t", t=PACK)
            parts = [sb([P, 2 * P * PACK], BF16, "%s%d" % (name, u)) for u in range(2)]
            for u, copy in enumerate(copies):
                copy(parts[u][:].rearrange("p (t m j) -> p m j t", t=2, j=PACK), src[:, :, :, 2 * u : 2 * u + 2])
            return parts

        w1_bf = cast_dealt(w1_raw, "w1_bf", (nc.scalar.copy, nc.vector.tensor_copy))
        w1_q = [quantize(w1_bf[0][:], "w1_0"), quantize(w1_bf[1][:], "w1_1", tag="w1_bf0")]
        w4_raw = load_weight(w4, "w4_raw", tag="w1_raw")
        w3_raw = load_weight(w3, "w3_raw", tag="w1_bf1")
        y_acc = []
        for t in range(PACK):
            acc = psum.tile([P, S], F32, name="y%d" % t, tag="bankA%d" % t)
            mm(acc[:], w1_q[t // 2], slice((t % 2) * P, (t % 2 + 1) * P), (xq_code, xq_scale), True, True)
            y_acc.append(acc)
        rl = {}

        def gained_relu(t, dst):
            rl[t] = dst
            nc.vector.tensor_scalar(dst, y_acc[t][:], 0.0, gn_t[:, t : t + 1], ALU.max, ALU.mult)

        rl0 = sb([P, S], F32, "rl0")
        gained_relu(0, rl0[:])
        w2_bf = cast_dealt(w2_raw, "w2_bf", (nc.vector.tensor_copy, nc.scalar.copy))
        w2_q = [quantize(w2_bf[u][:], "w2_%d" % u) for u in range(2)]
        rl1 = sb([P, S], F32, "rl1", tag="w2_bf0")
        rl23 = sb([P, 2, S], F32, "rl23", tag="w2_bf1")
        gained_relu(1, rl1[:])
        gained_relu(2, rl23[:, 0, :])
        gained_relu(3, rl23[:, 1, :])

        def scatter(ds, t, start, count, on_vector):
            lists = n1_t[:, start // 16 : (start + count) // 16]
            src = rl[t][:, start : start + count]
            if on_vector:
                nc.vector.tensor_copy(ds[:].indirect(lists), src)
            else:
                nc.scalar.activation(ds[:].indirect(lists), src, COPY)

        ds0 = sb([P, S], F32, "ds0", tag="w2_raw")
        scatter(ds0, 0, 0, HALF, False)
        scatter(ds0, 0, HALF, HALF, False)

        for t in range(PACK):
            acc = psum.tile([P, S], F32, name="d%d" % t, tag="bankB%d" % t)
            mm(acc[:], w2_q[t // 2], slice((t % 2) * P, (t % 2 + 1) * P), (xh_code, xh_scale), True, True)
            if t < 2:
                nc.vector.tensor_copy(d_win[t][:, 0:S], acc[:])
            else:
                nc.scalar.copy(d_win[t][:, 0:S], acc[:])

        def cast_plain(copy, bf, raw):
            copy(bf.rearrange("p (c i j) -> p c j i", i=2, j=PACK), raw.rearrange("p j (c i) -> p c j i", i=2))

        def gained_d(t):
            nc.vector.tensor_scalar(dg_win[t][:, 0:S], d_win[t][:, 0:S], gm75[:, t : t + 1], None, ALU.mult)

        for t in range(2):
            gained_d(t)
        w4_early_bf = sb([P, EARLY * PACK], BF16, "w4_early_bf")
        cast_plain(nc.vector.tensor_copy, w4_early_bf[:], w4_raw[:, :, 0:EARLY])
        for t in range(2, PACK):
            gained_d(t)
        w4_early_q = quantize(w4_early_bf[:], "w4_early")

        ab = sb([P, PACK, S], F32, "ab")
        ce = sb([P, PACK, S], F32, "ce")
        for t in range(PACK):
            for first, second, prod in ((n2_t, n3_t, ab), (n4_t, n5_t, ce)):
                left = ring.tile([P, S], F32, name="left", bufs=8, align_bytes=64)
                nc.scalar.activation(left[:], dg_win[t][:].indirect(first[:]), COPY)
                nc.vector.tensor_tensor(prod[:, t, :], d_win[t][:].indirect(second[:]), left[:], ALU.mult)

        w3_early_bf = ring.tile([P, EARLY * PACK], BF16, name="w3_early_bf", tag="left", bufs=8, align_bytes=64)
        cast_plain(nc.vector.tensor_copy, w3_early_bf[:], w3_raw[:, :, 0:EARLY])
        ds3 = sb([P, S], F32, "ds3", tag="dg_win3")
        scatter(ds3, 3, 0, SHARE, True)
        halves = [slice(u * HALF, (u + 1) * HALF) for u in range(2)]
        z2_bf = sb([P, S * PACK], BF16, "z2_bf")
        nc.vector.tensor_tensor(
            z2_bf[:].rearrange("p (c i t) -> p c t i", i=2, t=PACK),
            ab[:].rearrange("p t (c i) -> p c t i", i=2),
            ce[:].rearrange("p t (c i) -> p c t i", i=2),
            ALU.subtract,
        )
        w3_early_q = quantize(w3_early_bf[:], "w3_early")
        z2_code, z2_scale = quantize(z2_bf[:], "z2")
        z2_q = [(z2_code[:, cols], z2_scale[:, cols]) for cols in halves]

        zp = sb([P, PACK, S], BF16, "zp", tag="z2_bf")

        def z_plane(ds, t, cols):
            nc.vector.scalar_tensor_tensor(
                zp[:, t, cols], y_acc[t][:, cols], gn_half[:, t : t + 1], ds[:, cols], ALU.mult, ALU.add
            )

        ds1 = sb([P, S], F32, "ds1", tag="dg_win1")
        ds2 = sb([P, S], F32, "ds2", tag="dg_win2")
        scatter(ds1, 1, 0, HALF, False)
        scatter(ds1, 1, HALF, HALF, False)
        scatter(ds2, 2, 0, HALF, False)
        scatter(ds2, 2, HALF, HALF, False)
        scatter(ds3, 3, SHARE, S - SHARE, False)
        late_bf = sb([P, 2, (N - EARLY) * PACK], BF16, "late_bf", tag="w2_bf1")
        cast_plain(nc.scalar.copy, late_bf[:, 0, :], w4_raw[:, :, EARLY:N])
        cast_plain(nc.scalar.copy, late_bf[:, 1, :], w3_raw[:, :, EARLY:N])
        for t, ds in enumerate((ds0, ds1, ds2)):
            z_plane(ds, t, slice(0, S))
        for cols in halves:
            z_plane(ds3, 3, cols)
        z_bf = [sb([P, HALF * PACK], BF16, "z_bf%d" % u) for u in range(2)]
        for u in range(2):
            nc.vector.tensor_copy(
                z_bf[u][:].rearrange("p (c i t) -> p c t i", i=4, t=PACK),
                zp[:, :, halves[u]].rearrange("p t (c i) -> p c t i", i=4),
            )
        z_q = [quantize(z_bf[u][:], "z_%d" % u) for u in range(2)]
        late_q = quantize(late_bf[:].rearrange("p w c -> p (w c)"), "late", tag="z_bf1")

        accs = {}
        for m in range(PACK):
            for u in range(2):
                acc = psum.tile([P, HALF], F32, name="h%d_%d" % (m, u), tag="bank%s%d" % ("BA"[u], m))
                first = (m % 2) * P
                if m < 2:
                    mm(acc[:], w4_early_q, slice(first, first + P), z2_q[u], True, False)
                    mm(acc[:], w3_early_q, slice(first, first + P), z_q[u], False, True)
                else:
                    mm(acc[:], late_q, slice(first, first + P), z2_q[u], True, False)
                    mm(acc[:], late_q, slice(HALF + first, HALF + first + P), z_q[u], False, True)
                accs[m, u] = acc

        def leave(m, u, on_vector):
            if on_vector:
                nc.vector.tensor_copy(h_win[m][:, halves[u]], accs[m, u][:])
            else:
                nc.scalar.copy(h_win[m][:, halves[u]], accs[m, u][:])

        def fetch(m, start, count, on_vector):
            dst = members[m][:, start : start + count, :].rearrange("p j e -> p (j e)")
            lists = n6_t[:, start // 4 : (start + count) // 4]
            if on_vector:
                nc.vector.tensor_copy(dst, h_win[m][:].indirect(lists))
            else:
                nc.scalar.activation(dst, h_win[m][:].indirect(lists), COPY)

        def clip(m, start, count):
            cols = slice(start, start + count)
            mb = members[m][:, cols, :]
            hi2 = ring.tile([P, count, 2], F32, name="hi2", bufs=2)
            lo2 = ring.tile([P, count, 2], F32, name="lo2", bufs=2)
            mx = ring.tile([P, count], F32, name="mx", bufs=2)
            mn = ring.tile([P, count], F32, name="mn", bufs=2)
            cap = ring.tile([P, count], F32, name="cap", bufs=2)
            res = ring.tile([P, count], F32, name="res", bufs=3)
            nc.vector.tensor_tensor(hi2[:], mb[:, :, 0:2], mb[:, :, 2:4], ALU.max)
            nc.vector.tensor_tensor(lo2[:], mb[:, :, 0:2], mb[:, :, 2:4], ALU.min)
            nc.vector.tensor_tensor(mx[:], hi2[:, :, 0], hi2[:, :, 1], ALU.max)
            nc.vector.tensor_tensor(mn[:], lo2[:, :, 0], lo2[:, :, 1], ALU.min)
            nc.vector.scalar_tensor_tensor(cap[:], h_win[m][:, cols], 1.5, mx[:], ALU.mult, ALU.min)
            nc.vector.tensor_tensor(res[:], cap[:], mn[:], ALU.max)
            nc.sync.dma_start(out[m * P : (m + 1) * P, cols], res[:])

        members = [ring.tile([P, S, 4], F32, name="members%d" % m, tag="members", bufs=3) for m in range(PACK)]
        leave(0, 0, False)
        leave(0, 1, True)
        leave(1, 0, False)
        for m in range(PACK):
            for u in range(2):
                if m == 0 and u == 0:
                    fetch(m, 0, P, False)
                    fetch(m, P, P, True)
                    leave(1, 1, False)
                else:
                    fetch(m, u * HALF, HALF, False)
                if u == 0 and m in (1, 2):
                    leave(m + 1, 0, False)
                    leave(m + 1, 1, True)
                clip(m, u * HALF, HALF)
